import numpy as np
import ml_dtypes

BF16 = ml_dtypes.bfloat16


def bf(x):
    return np.asarray(x, np.float32).astype(BF16)


def f32(x):
    return np.asarray(x, np.float32)


def f64(x):
    return np.asarray(x).astype(np.float64)


def striped(idx):
    return np.tile(idx.reshape(-1, 16).T, (8, 1))


S, K, M, N, D, V = 512, 128, 128, 512, 4, 128


def setup_inputs():
    return {"table": bf(np.random.standard_normal((K, S))), "w": bf(np.random.standard_normal((K, M)) / np.sqrt(D * K)), "s": f32(0.5 + np.random.random_sample((M, 1))), "b": f32(0.5 * np.random.standard_normal((M, 1))), "offs": striped(np.random.permutation(np.tile(np.arange(S), 2))[:N])}


def reference(table, w, s, b, offs):
    idx = offs[:16].T.reshape(-1)
    x = f64(table)[:, idx]
    y = f64(w).T @ sum(x[:, t * V : (t + 1) * V] for t in range(D))
    return y * f64(s) + f64(b)

@@ -1,0 +1,41 @@
+import concourse.mybir as mybir
+
+BF16, F32, U16 = mybir.dt.bfloat16, mybir.dt.float32, mybir.dt.uint16
+MULT, ADD = mybir.AluOpType.mult, mybir.AluOpType.add
+
+K = 128
+M = 128
+S = 512
+V = 128
+D = 4
+COLS = V // 16
+
+FLOPS = (D - 1) * K * V + 2 * K * M * V + 2 * M * V
+
+
+def tile_gather_matmul_kernel(tc, table, w, s, b, offs, out):
+    nc = tc.nc
+    with (
+        tc.tile_pool(name="held", bufs=1) as held,
+        tc.psum_pool(name="psum", bufs=1) as psum,
+    ):
+        offsets = held.tile([128, D * COLS], U16, name="offsets")
+        nodes = held.tile([K, S], BF16, name="nodes")
+        weights = held.tile([K, M], BF16, name="weights")
+        gain = held.tile([M, 1], F32, name="gain")
+        shift = held.tile([M, 1], F32, name="shift")
+
+        nc.sync.dma_start(offsets[:], offs)
+        nc.scalar.dma_start(nodes[:], table)
+        nc.sync.dma_start(weights[:], w)
+        nc.gpsimd.dma_start(gain[:], s)
+        nc.gpsimd.dma_start(shift[:], b)
+
+        projected = psum.tile([M, V], F32, name="projected")
+        for t in range(D):
+            neighbour = nodes[:].indirect(offsets[:, t * COLS : (t + 1) * COLS])
+            nc.tensor.matmul(projected[:], weights[:], neighbour, start=(t == 0), stop=(t == D - 1))
+
+        result = held.tile([M, V], F32, name="result")
+        nc.vector.tensor_scalar(result[:], projected[:], gain[:], shift[:], MULT, ADD)
+        nc.sync.dma_start(out, result[:])

@@ -28,8 +28,8 @@ def tile_gather_matmul_kernel(tc, table, w, s, b, offs, out):
         nc.sync.dma_start(offsets[:], offs)
         nc.scalar.dma_start(nodes[:], table)
         nc.sync.dma_start(weights[:], w)
-        nc.gpsimd.dma_start(gain[:], s)
-        nc.gpsimd.dma_start(shift[:], b)
+        nc.scalar.dma_start(gain[:], s)
+        nc.sync.dma_start(shift[:], b)
 
         projected = psum.tile([M, V], F32, name="projected")
         for t in range(D):

@@ -25,9 +25,9 @@ def tile_gather_matmul_kernel(tc, table, w, s, b, offs, out):
         gain = held.tile([M, 1], F32, name="gain")
         shift = held.tile([M, 1], F32, name="shift")
 
+        nc.sync.dma_start(nodes[:], table)
+        nc.scalar.dma_start(weights[:], w)
         nc.sync.dma_start(offsets[:], offs)
-        nc.scalar.dma_start(nodes[:], table)
-        nc.sync.dma_start(weights[:], w)
         nc.scalar.dma_start(gain[:], s)
         nc.sync.dma_start(shift[:], b)
 

@@ -9,6 +9,7 @@ S = 512
 V = 128
 D = 4
 COLS = V // 16
+ROW_GRID = 256
 
 FLOPS = (D - 1) * K * V + 2 * K * M * V + 2 * M * V
 
@@ -20,8 +21,9 @@ def tile_gather_matmul_kernel(tc, table, w, s, b, offs, out):
         tc.psum_pool(name="psum", bufs=1) as psum,
     ):
         offsets = held.tile([128, D * COLS], U16, name="offsets")
-        nodes = held.tile([K, S], BF16, name="nodes")
-        weights = held.tile([K, M], BF16, name="weights")
+        nodes = held.tile([K, S], BF16, name="nodes", align_bytes=ROW_GRID)
+        weights = held.tile([K, M], BF16, name="weights", align_bytes=ROW_GRID)
+        result = held.tile([M, V], F32, name="result", align_bytes=ROW_GRID)
         gain = held.tile([M, 1], F32, name="gain")
         shift = held.tile([M, 1], F32, name="shift")
 
@@ -36,6 +38,5 @@ def tile_gather_matmul_kernel(tc, table, w, s, b, offs, out):
             neighbour = nodes[:].indirect(offsets[:, t * COLS : (t + 1) * COLS])
             nc.tensor.matmul(projected[:], weights[:], neighbour, start=(t == 0), stop=(t == D - 1))
 
-        result = held.tile([M, V], F32, name="result")
         nc.vector.tensor_scalar(result[:], projected[:], gain[:], shift[:], MULT, ADD)
         nc.sync.dma_start(out, result[:])

@@ -10,6 +10,8 @@ V = 128
 D = 4
 COLS = V // 16
 ROW_GRID = 256
+BANK = 512
+WARM_UPS = 3
 
 FLOPS = (D - 1) * K * V + 2 * K * M * V + 2 * M * V
 
@@ -32,6 +34,13 @@ def tile_gather_matmul_kernel(tc, table, w, s, b, offs, out):
         nc.sync.dma_start(offsets[:], offs)
         nc.scalar.dma_start(gain[:], s)
         nc.sync.dma_start(shift[:], b)
+
+        zeros = held.tile([K, M], BF16, name="zeros")
+        nc.vector.memset(zeros[:], 0.0)
+        unread = psum.tile([M, BANK], F32, name="unread")
+        zeros_bank_wide = zeros[:].unsqueeze(1).to_broadcast([K, BANK // M, M])
+        for i in range(WARM_UPS):
+            nc.tensor.matmul(unread[:], zeros[:], zeros_bank_wide, start=True, stop=True)
 
         projected = psum.tile([M, V], F32, name="projected")
         for t in range(D):

@@ -32,7 +32,7 @@ def tile_gather_matmul_kernel(tc, table, w, s, b, offs, out):
         nc.sync.dma_start(nodes[:], table)
         nc.scalar.dma_start(weights[:], w)
         nc.sync.dma_start(offsets[:], offs)
-        nc.scalar.dma_start(gain[:], s)
+        nc.sync.dma_start(gain[:], s)
         nc.sync.dma_start(shift[:], b)
 
         zeros = held.tile([K, M], BF16, name="zeros")

@@ -30,7 +30,7 @@ def tile_gather_matmul_kernel(tc, table, w, s, b, offs, out):
         shift = held.tile([M, 1], F32, name="shift")
 
         nc.sync.dma_start(nodes[:], table)
-        nc.scalar.dma_start(weights[:], w)
+        nc.sync.dma_start(weights[:], w)
         nc.sync.dma_start(offsets[:], offs)
         nc.sync.dma_start(gain[:], s)
         nc.sync.dma_start(shift[:], b)

@@ -10,8 +10,6 @@ V = 128
 D = 4
 COLS = V // 16
 ROW_GRID = 256
-BANK = 512
-WARM_UPS = 3
 
 FLOPS = (D - 1) * K * V + 2 * K * M * V + 2 * M * V
 
@@ -34,13 +32,6 @@ def tile_gather_matmul_kernel(tc, table, w, s, b, offs, out):
         nc.sync.dma_start(offsets[:], offs)
         nc.sync.dma_start(gain[:], s)
         nc.sync.dma_start(shift[:], b)
-
-        zeros = held.tile([K, M], BF16, name="zeros")
-        nc.vector.memset(zeros[:], 0.0)
-        unread = psum.tile([M, BANK], F32, name="unread")
-        zeros_bank_wide = zeros[:].unsqueeze(1).to_broadcast([K, BANK // M, M])
-        for i in range(WARM_UPS):
-            nc.tensor.matmul(unread[:], zeros[:], zeros_bank_wide, start=True, stop=True)
 
         projected = psum.tile([M, V], F32, name="projected")
         for t in range(D):

@@ -9,6 +9,7 @@ S = 512
 V = 128
 D = 4
 COLS = V // 16
+BLOCK = 32
 ROW_GRID = 256
 
 FLOPS = (D - 1) * K * V + 2 * K * M * V + 2 * M * V
@@ -24,19 +25,22 @@ def tile_gather_matmul_kernel(tc, table, w, s, b, offs, out):
         nodes = held.tile([K, S], BF16, name="nodes", align_bytes=ROW_GRID)
         weights = held.tile([K, M], BF16, name="weights", align_bytes=ROW_GRID)
         result = held.tile([M, V], F32, name="result", align_bytes=ROW_GRID)
-        gain = held.tile([M, 1], F32, name="gain")
-        shift = held.tile([M, 1], F32, name="shift")
+        affine_rows = held.tile([M, BLOCK], F32, name="affine_rows", align_bytes=64)
+        affine_columns = held.tile([M, BLOCK], F32, name="affine_columns", align_bytes=64)
+        nc.vector.memset(affine_rows[:], 0.0)
 
         nc.sync.dma_start(nodes[:], table)
         nc.sync.dma_start(weights[:], w)
         nc.sync.dma_start(offsets[:], offs)
-        nc.sync.dma_start(gain[:], s)
-        nc.sync.dma_start(shift[:], b)
+        nc.sync.dma_start(affine_rows[0:M:BLOCK, :], s.rearrange("(a p) o -> a (p o)", p=BLOCK))
+        nc.sync.dma_start(affine_rows[1:M:BLOCK, :], b.rearrange("(a p) o -> a (p o)", p=BLOCK))
 
         projected = psum.tile([M, V], F32, name="projected")
         for t in range(D):
             neighbour = nodes[:].indirect(offsets[:, t * COLS : (t + 1) * COLS])
             nc.tensor.matmul(projected[:], weights[:], neighbour, start=(t == 0), stop=(t == D - 1))
 
-        nc.vector.tensor_scalar(result[:], projected[:], gain[:], shift[:], MULT, ADD)
+        nc.vector.transpose(affine_columns[:], affine_rows[:])
+        gain, shift = affine_columns[:, 0:1], affine_columns[:, 1:2]
+        nc.vector.tensor_scalar(result[:], projected[:], gain, shift, MULT, ADD)
         nc.sync.dma_start(out, result[:])

import concourse.mybir as mybir

BF16, F32, U16 = mybir.dt.bfloat16, mybir.dt.float32, mybir.dt.uint16
MULT, ADD = mybir.AluOpType.mult, mybir.AluOpType.add

K = 128
M = 128
S = 512
V = 128
D = 4
COLS = V // 16
BLOCK = 32
ROW_GRID = 256

FLOPS = (D - 1) * K * V + 2 * K * M * V + 2 * M * V


def tile_gather_matmul_kernel(tc, table, w, s, b, offs, out):
    nc = tc.nc
    with (
        tc.tile_pool(name="held", bufs=1) as held,
        tc.psum_pool(name="psum", bufs=1) as psum,
    ):
        offsets = held.tile([128, D * COLS], U16, name="offsets")
        nodes = held.tile([K, S], BF16, name="nodes", align_bytes=ROW_GRID)
        weights = held.tile([K, M], BF16, name="weights", align_bytes=ROW_GRID)
        result = held.tile([M, V], F32, name="result", align_bytes=ROW_GRID)
        affine_rows = held.tile([M, BLOCK], F32, name="affine_rows", align_bytes=64)
        affine_columns = held.tile([M, BLOCK], F32, name="affine_columns", align_bytes=64)
        nc.vector.memset(affine_rows[:], 0.0)

        nc.sync.dma_start(nodes[:], table)
        nc.sync.dma_start(weights[:], w)
        nc.sync.dma_start(offsets[:], offs)
        nc.sync.dma_start(affine_rows[0:M:BLOCK, :], s.rearrange("(a p) o -> a (p o)", p=BLOCK))
        nc.sync.dma_start(affine_rows[1:M:BLOCK, :], b.rearrange("(a p) o -> a (p o)", p=BLOCK))

        projected = psum.tile([M, V], F32, name="projected")
        for t in range(D):
            neighbour = nodes[:].indirect(offsets[:, t * COLS : (t + 1) * COLS])
            nc.tensor.matmul(projected[:], weights[:], neighbour, start=(t == 0), stop=(t == D - 1))

        nc.vector.transpose(affine_columns[:], affine_rows[:])
        gain, shift = affine_columns[:, 0:1], affine_columns[:, 1:2]
        nc.vector.tensor_scalar(result[:], projected[:], gain, shift, MULT, ADD)
        nc.sync.dma_start(out, result[:])
